import numpy as np
import ml_dtypes


def mxq(x, axis, fmt="e4m3"):
    dtype, down = {"e4m3": (ml_dtypes.float8_e4m3fn, 7), "e5m2": (ml_dtypes.float8_e5m2, 14)}[fmt]
    v = np.moveaxis(np.asarray(x, np.float32).astype(ml_dtypes.bfloat16).astype(np.float64), axis, -1)
    blocks = v.reshape(v.shape[:-1] + (-1, 32))
    amax = np.abs(blocks).max(-1, keepdims=True)
    byte = np.maximum(np.where(amax > 0, np.frexp(amax)[1] - 1 + 127, 0) - down, 1)
    scale = np.exp2(byte - 127.0)
    codes = (blocks / scale).astype(np.float32).astype(dtype).astype(np.float64)
    return np.moveaxis((codes * scale).reshape(v.shape), -1, axis)


WIDE = False


def mx_kscale(k):
    if not WIDE:
        return np.ones(k)
    levels = np.array([10, -10, 5, -5, 0])
    if k % 512:
        return np.exp2(np.random.permutation(np.resize(levels, k // 32))).repeat(32)
    a = np.empty((k // 512, 16))
    for p in range(k // 512):
        a[p, :8] = np.random.permutation(np.resize(levels, 8))
        for g in range(8):
            far = levels[np.abs(levels - a[p, g]) >= 10]
            a[p, g + 8] = far[np.random.randint(len(far))]
    return np.exp2(a.ravel()).repeat(32)


def f64(x):
    return np.asarray(x).astype(np.float64)


def striped(idx):
    return np.tile(idx.reshape(-1, 16).T, (8, 1)).astype(np.uint16)


def unstriped(offs):
    return offs[:16].T.reshape(-1).astype(np.int64)


def pack_weight(w):
    k, n = w.shape
    w = f64(np.asarray(w, np.float32).astype(ml_dtypes.bfloat16)).reshape(k // 32, 32, n)
    amax = np.abs(w).max(1)
    byte = np.clip(np.where(amax > 0, np.frexp(amax)[1] - 1 + 127 - 7, 1), 1, 254)
    scaled = (w * np.exp2(127.0 - byte)[:, None, :]).reshape(k, n).astype(np.float32)
    words = np.ascontiguousarray(scaled.reshape(k // 512, 128, 4, n).transpose(0, 1, 3, 2)).astype(ml_dtypes.float8_e4m3fn).view(np.uint8)
    return words, np.ascontiguousarray(byte.astype(np.uint8).reshape(k // 512, 16, n))


def unpack_weight(words, scales):
    g, p, n, _ = words.shape
    vals = np.ascontiguousarray(words).view(ml_dtypes.float8_e4m3fn).astype(np.float64) * np.repeat(np.exp2(scales.astype(np.float64) - 127.0), 8, axis=1)[..., None]
    return vals.transpose(0, 1, 3, 2).reshape(g * 512, n)


def sigmoid(v):
    return 1.0 / (1.0 + np.exp(-np.maximum(v, -700.0)))


K, T, S, N = 1024, 2048, 512, 128
P = 2 ** 7


def setup_inputs():
    n = np.random.standard_normal
    s = mx_kscale(K)[:, None]
    packed_xT = pack_weight(n((K, T)) * s)
    return {
        "x_words": packed_xT[0],
        "x_scales": packed_xT[1],
        "w1": (n((K, N)) / np.sqrt(K) / s).astype(np.float32),
        "w2": (n((K, N)) / np.sqrt(K) / s).astype(np.float32),
        "w3": (n((K, N)) / np.sqrt(K) / s).astype(np.float32),
        "buys": (np.tile((np.random.uniform(size=S) < 0.5) * 1.0, (P, 1))).astype(np.float32),
        "logv": (n((N, S))).astype(np.float32),
        "offs": striped(np.random.permutation(T)[:S]),
    }


def reference(x_words, x_scales, w1, w2, w3, buys, logv, offs):
    xq = unpack_weight(x_words, x_scales)[:, unstriped(offs)]
    yp = mxq(f64(w1), 0, "e4m3").T @ xq
    ym = mxq(f64(w2), 0, "e4m3").T @ xq
    ys = mxq(f64(w3), 0, "e4m3").T @ xq
    sg = 0.7 * (np.log(np.exp(ys) + 1.0)) + 0.3
    return sigmoid(yp) * (np.exp(0.5 * ym + 0.125 * ((sg) ** 2))) - (f64(buys)[:1] * (np.exp(0.5 * f64(logv))))

@@ -1,0 +1,147 @@
+import math
+from contextlib import ExitStack
+
+import concourse.mybir as mybir
+
+K, T, S, N = 1024, 2048, 512, 128
+FLOPS = 3 * 2 * K * S * N
+
+F32 = mybir.dt.float32
+BF16 = mybir.dt.bfloat16
+I32 = mybir.dt.int32
+U32 = mybir.dt.uint32
+U16 = mybir.dt.uint16
+U8 = mybir.dt.uint8
+FP8X4 = mybir.dt.float8_e4m3fn_x4
+ACT = mybir.ActivationFunctionType
+ALU = mybir.AluOpType
+
+P = 128
+PACK = 4
+PASSES = K // (P * PACK)
+HALF = S // 2
+TAIL = ((0, 256), (256, 384), (384, 512))
+
+SQ = 0.125 * 0.7 * 0.7
+LIN = 2.0 * 0.3 / 0.7
+OUT_SCALE = 0.5 * math.e ** (0.125 * 0.3 * 0.3)
+
+
+def tile_picked_yziln_exp_p_kernel(tc, x_words, x_scales, w1, w2, w3, buys, logv, offs, out):
+    nc = tc.nc
+    with ExitStack() as ctx:
+        sb = ctx.enter_context(tc.tile_pool(name="sb", bufs=1))
+        ps = ctx.enter_context(tc.psum_pool(name="ps", bufs=1))
+
+        offsets = sb.tile([P, S // 16], U16, name="offsets")
+
+        def load_weight(w, name, tag):
+            raw = sb.tile([P, PASSES, PACK * N], F32, name=name + "_raw", tag=tag, align_bytes=64)
+            nc.sync.dma_start(raw[:], w.rearrange("(g p j) n -> p g (j n)", g=PASSES, j=PACK))
+            return raw
+
+        def quantise_weight(raw, name, tag):
+            grouped = sb.tile([P, PASSES * N * PACK], BF16, name=name + "_bf", tag=tag, align_bytes=64)
+            codes = sb.tile([P, PASSES * N], U32, name=name + "_codes", align_bytes=64)
+            scales = sb.tile([P, PASSES * N], U8, name=name + "_scales", align_bytes=64)
+            nc.vector.tensor_copy(
+                grouped[:].rearrange("p (g c i j) -> p g c j i", g=PASSES, i=4, j=PACK),
+                raw[:].rearrange("p g (j c i) -> p g c j i", j=PACK, i=4),
+            )
+            nc.vector.quantize_mx(out=codes[:].bitcast(FP8X4), scales=scales[:], in_=grouped[:])
+            return codes, scales
+
+        scale_table = sb.tile([P, T], U8, name="scale_table", tag="slot_c", align_bytes=64)
+        nc.vector.memset(scale_table[:].bitcast(I32), 0)
+        for q in range(4):
+            nc.scalar.dma_start(
+                scale_table[32 * q : 32 * q + 4 * PASSES, :].bitcast(I32),
+                x_scales[:, 4 * q : 4 * q + 4, :].bitcast(I32),
+            )
+
+        w3_raw = load_weight(w3, "w3", "slot_a")
+        nc.sync.dma_start(offsets[:], offs)
+        word_tables = []
+        for g in range(PASSES):
+            table = sb.tile([P, T], I32, name="word_table%d" % g, tag="slot_table%d" % g, align_bytes=64)
+            nc.sync.dma_start(table[:], x_words[g].rearrange("p n t -> p (n t)").bitcast(I32))
+            word_tables.append(table)
+        logv_sb = sb.tile([P, S], F32, name="logv_sb")
+        nc.sync.dma_start(logv_sb[:], logv)
+
+        w3_q = quantise_weight(w3_raw, "w3", "slot_b")
+        w2_raw = load_weight(w2, "w2", "slot_a")
+        buys_sb = sb.tile([P, S], F32, name="buys_sb", tag="slot_b", align_bytes=64)
+        nc.sync.dma_start(buys_sb[:], buys)
+        x_planes = sb.tile([P, S], U8, name="x_planes", align_bytes=64)
+        nc.vector.tensor_copy(x_planes[:], scale_table[:].indirect(offsets[:]))
+        x_codes = [
+            sb.tile([P, S], U32, name="x_codes0", tag="slot_c", align_bytes=64),
+            sb.tile([P, S], U32, name="x_codes1", align_bytes=64),
+        ]
+
+        def product_pass(acc, w_q, g, lo, hi):
+            codes, scales = w_q
+            nc.tensor.matmul_mx(
+                out=acc,
+                lhsT=codes[:, g * N : (g + 1) * N].bitcast(FP8X4),
+                lhsT_scale=scales[:, g * N : (g + 1) * N],
+                rhs=x_codes[g][:, lo:hi].bitcast(FP8X4),
+                rhs_scale=x_planes[4 * g : P, lo:hi],
+                start=(g == 0),
+                stop=(g == PASSES - 1),
+            )
+
+        ys = [ps.tile([P, HALF], F32, name="ys%d" % h) for h in range(2)]
+        nc.vector.tensor_copy(x_codes[0][:], word_tables[0][:].bitcast(U32).indirect(offsets[:]))
+        w1_raw = load_weight(w1, "w1", "slot_table0")
+        for h in range(2):
+            product_pass(ys[h][:], w3_q, 0, h * HALF, (h + 1) * HALF)
+
+        spent = sb.tile([P, S], F32, name="spent")
+        nc.scalar.activation(spent[:], logv_sb[:], ACT.Exp, scale=0.5)
+
+        exp_ys = sb.tile([P, S], F32, name="exp_ys")
+        for h in range(2):
+            lo, hi = h * HALF, (h + 1) * HALF
+            nc.vector.tensor_copy(
+                x_codes[1][:, lo:hi],
+                word_tables[1][:].bitcast(U32).indirect(offsets[:, lo // 16 : hi // 16]),
+            )
+            product_pass(ys[h][:], w3_q, 1, lo, hi)
+            nc.scalar.activation(exp_ys[:, lo:hi], ys[h][:], ACT.Exp)
+
+        softplus = logv_sb
+        nc.scalar.activation(softplus[:], exp_ys[:], ACT.Ln, bias=1.0)
+
+        ym = ps.tile([P, S], F32, name="ym")
+        w2_q = quantise_weight(w2_raw, "w2", "slot_table1")
+        for g in range(PASSES):
+            product_pass(ym[:], w2_q, g, 0, S)
+        yp = ps.tile([P, S], F32, name="yp")
+        w1_q = quantise_weight(w1_raw, "w1", "slot_table1")
+        for g in range(PASSES):
+            product_pass(yp[:], w1_q, g, 0, S)
+
+        quad = sb.tile([P, S], F32, name="quad")
+        expo = sb.tile([P, S], F32, name="expo")
+        halves = [slice(h * HALF, (h + 1) * HALF) for h in range(2)]
+        for c in halves:
+            nc.vector.scalar_tensor_tensor(quad[:, c], softplus[:, c], LIN, softplus[:, c], ALU.add, ALU.mult)
+        for c in halves:
+            nc.vector.scalar_tensor_tensor(expo[:, c], ym[:, c], 0.5 / SQ, quad[:, c], ALU.mult, ALU.add)
+
+        seen = sb.tile([P, S], F32, name="seen")
+        nc.vector.tensor_tensor(seen[:], spent[:], buys_sb[:], ALU.mult)
+
+        gate = sb.tile([P, S], F32, name="gate")
+        value = sb.tile([P, S], F32, name="value")
+        gated = sb.tile([P, S], F32, name="gated")
+        result = sb.tile([P, S], F32, name="result")
+        for lo, hi in TAIL:
+            c = slice(lo, hi)
+            nc.scalar.activation(gate[:, c], yp[:, c], ACT.Tanh, scale=0.5)
+            nc.scalar.activation(value[:, c], expo[:, c], ACT.Exp, scale=SQ)
+            nc.vector.scalar_tensor_tensor(gated[:, c], gate[:, c], 1.0, value[:, c], ALU.add, ALU.mult)
+            nc.vector.scalar_tensor_tensor(result[:, c], gated[:, c], OUT_SCALE, seen[:, c], ALU.mult, ALU.subtract)
+            nc.sync.dma_start(out[:, c], result[:, c])

@@ -20,7 +20,8 @@ P = 128
 PACK = 4
 PASSES = K // (P * PACK)
 HALF = S // 2
-TAIL = ((0, 256), (256, 384), (384, 512))
+TAIL = ((0, 128), (128, 256), (256, 384), (384, 512))
+YS_PIECES = (((0, 256),), ((256, 384), (384, 512)))
 
 SQ = 0.125 * 0.7 * 0.7
 LIN = 2.0 * 0.3 / 0.7
@@ -40,11 +41,11 @@ def tile_picked_yziln_exp_p_kernel(tc, x_words, x_scales, w1, w2, w3, buys, logv
             nc.sync.dma_start(raw[:], w.rearrange("(g p j) n -> p g (j n)", g=PASSES, j=PACK))
             return raw
 
-        def quantise_weight(raw, name, tag):
+        def quantise_weight(raw, name, tag, copy):
             grouped = sb.tile([P, PASSES * N * PACK], BF16, name=name + "_bf", tag=tag, align_bytes=64)
             codes = sb.tile([P, PASSES * N], U32, name=name + "_codes", align_bytes=64)
             scales = sb.tile([P, PASSES * N], U8, name=name + "_scales", align_bytes=64)
-            nc.vector.tensor_copy(
+            copy(
                 grouped[:].rearrange("p (g c i j) -> p g c j i", g=PASSES, i=4, j=PACK),
                 raw[:].rearrange("p g (j c i) -> p g c j i", j=PACK, i=4),
             )
@@ -53,13 +54,13 @@ def tile_picked_yziln_exp_p_kernel(tc, x_words, x_scales, w1, w2, w3, buys, logv
 
         scale_table = sb.tile([P, T], U8, name="scale_table", tag="slot_c", align_bytes=64)
         nc.vector.memset(scale_table[:].bitcast(I32), 0)
+        w3_raw = load_weight(w3, "w3", "slot_a")
         for q in range(4):
-            nc.scalar.dma_start(
+            nc.sync.dma_start(
                 scale_table[32 * q : 32 * q + 4 * PASSES, :].bitcast(I32),
                 x_scales[:, 4 * q : 4 * q + 4, :].bitcast(I32),
             )
 
-        w3_raw = load_weight(w3, "w3", "slot_a")
         nc.sync.dma_start(offsets[:], offs)
         word_tables = []
         for g in range(PASSES):
@@ -69,16 +70,11 @@ def tile_picked_yziln_exp_p_kernel(tc, x_words, x_scales, w1, w2, w3, buys, logv
         logv_sb = sb.tile([P, S], F32, name="logv_sb")
         nc.sync.dma_start(logv_sb[:], logv)
 
-        w3_q = quantise_weight(w3_raw, "w3", "slot_b")
+        w3_q = quantise_weight(w3_raw, "w3", "slot_b", nc.scalar.copy)
         w2_raw = load_weight(w2, "w2", "slot_a")
-        buys_sb = sb.tile([P, S], F32, name="buys_sb", tag="slot_b", align_bytes=64)
-        nc.sync.dma_start(buys_sb[:], buys)
+        w1_raw = load_weight(w1, "w1", "slot_b")
         x_planes = sb.tile([P, S], U8, name="x_planes", align_bytes=64)
-        nc.vector.tensor_copy(x_planes[:], scale_table[:].indirect(offsets[:]))
-        x_codes = [
-            sb.tile([P, S], U32, name="x_codes0", tag="slot_c", align_bytes=64),
-            sb.tile([P, S], U32, name="x_codes1", align_bytes=64),
-        ]
+        x_codes = [sb.tile([P, S], U32, name="x_codes0", align_bytes=64)]
 
         def product_pass(acc, w_q, g, lo, hi):
             codes, scales = w_q
@@ -92,15 +88,19 @@ def tile_picked_yziln_exp_p_kernel(tc, x_words, x_scales, w1, w2, w3, buys, logv
                 stop=(g == PASSES - 1),
             )
 
-        ys = [ps.tile([P, HALF], F32, name="ys%d" % h) for h in range(2)]
+        ys = {lo: ps.tile([P, hi - lo], F32, name="ys%d" % lo) for half in YS_PIECES for lo, hi in half}
         nc.vector.tensor_copy(x_codes[0][:], word_tables[0][:].bitcast(U32).indirect(offsets[:]))
-        w1_raw = load_weight(w1, "w1", "slot_table0")
-        for h in range(2):
-            product_pass(ys[h][:], w3_q, 0, h * HALF, (h + 1) * HALF)
+        nc.vector.tensor_copy(x_planes[:], scale_table[:].indirect(offsets[:]))
+        buys_sb = sb.tile([P, S], F32, name="buys_sb", tag="slot_table0", align_bytes=64)
+        nc.sync.dma_start(buys_sb[:], buys)
+        for half in YS_PIECES:
+            for lo, hi in half:
+                product_pass(ys[lo][:], w3_q, 0, lo, hi)
 
         spent = sb.tile([P, S], F32, name="spent")
         nc.scalar.activation(spent[:], logv_sb[:], ACT.Exp, scale=0.5)
 
+        x_codes.append(sb.tile([P, S], U32, name="x_codes1", tag="slot_c", align_bytes=64))
         exp_ys = sb.tile([P, S], F32, name="exp_ys")
         for h in range(2):
             lo, hi = h * HALF, (h + 1) * HALF
@@ -108,22 +108,23 @@ def tile_picked_yziln_exp_p_kernel(tc, x_words, x_scales, w1, w2, w3, buys, logv
                 x_codes[1][:, lo:hi],
                 word_tables[1][:].bitcast(U32).indirect(offsets[:, lo // 16 : hi // 16]),
             )
-            product_pass(ys[h][:], w3_q, 1, lo, hi)
-            nc.scalar.activation(exp_ys[:, lo:hi], ys[h][:], ACT.Exp)
+            for lo, hi in YS_PIECES[h]:
+                product_pass(ys[lo][:], w3_q, 1, lo, hi)
+                nc.scalar.activation(exp_ys[:, lo:hi], ys[lo][:], ACT.Exp)
 
         softplus = logv_sb
         nc.scalar.activation(softplus[:], exp_ys[:], ACT.Ln, bias=1.0)
 
         ym = ps.tile([P, S], F32, name="ym")
-        w2_q = quantise_weight(w2_raw, "w2", "slot_table1")
+        w2_q = quantise_weight(w2_raw, "w2", "slot_table1", nc.vector.tensor_copy)
         for g in range(PASSES):
             product_pass(ym[:], w2_q, g, 0, S)
         yp = ps.tile([P, S], F32, name="yp")
-        w1_q = quantise_weight(w1_raw, "w1", "slot_table1")
+        w1_q = quantise_weight(w1_raw, "w1", "slot_table1", nc.vector.tensor_copy)
         for g in range(PASSES):
             product_pass(yp[:], w1_q, g, 0, S)
 
-        quad = sb.tile([P, S], F32, name="quad")
+        quad = sb.tile([P, S], F32, name="quad", tag="slot_table1", align_bytes=64)
         expo = sb.tile([P, S], F32, name="expo")
         halves = [slice(h * HALF, (h + 1) * HALF) for h in range(2)]
         for c in halves:
@@ -131,7 +132,7 @@ def tile_picked_yziln_exp_p_kernel(tc, x_words, x_scales, w1, w2, w3, buys, logv
         for c in halves:
             nc.vector.scalar_tensor_tensor(expo[:, c], ym[:, c], 0.5 / SQ, quad[:, c], ALU.mult, ALU.add)
 
-        seen = sb.tile([P, S], F32, name="seen")
+        seen = sb.tile([P, S], F32, name="seen", tag="slot_table1", align_bytes=64)
         nc.vector.tensor_tensor(seen[:], spent[:], buys_sb[:], ALU.mult)
 
         gate = sb.tile([P, S], F32, name="gate")

import math
from contextlib import ExitStack

import concourse.mybir as mybir

K, T, S, N = 1024, 2048, 512, 128
FLOPS = 3 * 2 * K * S * N

F32 = mybir.dt.float32
BF16 = mybir.dt.bfloat16
I32 = mybir.dt.int32
U32 = mybir.dt.uint32
U16 = mybir.dt.uint16
U8 = mybir.dt.uint8
FP8X4 = mybir.dt.float8_e4m3fn_x4
ACT = mybir.ActivationFunctionType
ALU = mybir.AluOpType

P = 128
PACK = 4
PASSES = K // (P * PACK)
HALF = S // 2
TAIL = ((0, 128), (128, 256), (256, 384), (384, 512))
YS_PIECES = (((0, 256),), ((256, 384), (384, 512)))

SQ = 0.125 * 0.7 * 0.7
LIN = 2.0 * 0.3 / 0.7
OUT_SCALE = 0.5 * math.e ** (0.125 * 0.3 * 0.3)


def tile_picked_yziln_exp_p_kernel(tc, x_words, x_scales, w1, w2, w3, buys, logv, offs, out):
    nc = tc.nc
    with ExitStack() as ctx:
        sb = ctx.enter_context(tc.tile_pool(name="sb", bufs=1))
        ps = ctx.enter_context(tc.psum_pool(name="ps", bufs=1))

        offsets = sb.tile([P, S // 16], U16, name="offsets")

        def load_weight(w, name, tag):
            raw = sb.tile([P, PASSES, PACK * N], F32, name=name + "_raw", tag=tag, align_bytes=64)
            nc.sync.dma_start(raw[:], w.rearrange("(g p j) n -> p g (j n)", g=PASSES, j=PACK))
            return raw

        def quantise_weight(raw, name, tag, copy):
            grouped = sb.tile([P, PASSES * N * PACK], BF16, name=name + "_bf", tag=tag, align_bytes=64)
            codes = sb.tile([P, PASSES * N], U32, name=name + "_codes", align_bytes=64)
            scales = sb.tile([P, PASSES * N], U8, name=name + "_scales", align_bytes=64)
            copy(
                grouped[:].rearrange("p (g c i j) -> p g c j i", g=PASSES, i=4, j=PACK),
                raw[:].rearrange("p g (j c i) -> p g c j i", j=PACK, i=4),
            )
            nc.vector.quantize_mx(out=codes[:].bitcast(FP8X4), scales=scales[:], in_=grouped[:])
            return codes, scales

        scale_table = sb.tile([P, T], U8, name="scale_table", tag="slot_c", align_bytes=64)
        nc.vector.memset(scale_table[:].bitcast(I32), 0)
        w3_raw = load_weight(w3, "w3", "slot_a")
        for q in range(4):
            nc.sync.dma_start(
                scale_table[32 * q : 32 * q + 4 * PASSES, :].bitcast(I32),
                x_scales[:, 4 * q : 4 * q + 4, :].bitcast(I32),
            )

        nc.sync.dma_start(offsets[:], offs)
        word_tables = []
        for g in range(PASSES):
            table = sb.tile([P, T], I32, name="word_table%d" % g, tag="slot_table%d" % g, align_bytes=64)
            nc.sync.dma_start(table[:], x_words[g].rearrange("p n t -> p (n t)").bitcast(I32))
            word_tables.append(table)
        logv_sb = sb.tile([P, S], F32, name="logv_sb")
        nc.sync.dma_start(logv_sb[:], logv)

        w3_q = quantise_weight(w3_raw, "w3", "slot_b", nc.scalar.copy)
        w2_raw = load_weight(w2, "w2", "slot_a")
        w1_raw = load_weight(w1, "w1", "slot_b")
        x_planes = sb.tile([P, S], U8, name="x_planes", align_bytes=64)
        x_codes = [sb.tile([P, S], U32, name="x_codes0", align_bytes=64)]

        def product_pass(acc, w_q, g, lo, hi):
            codes, scales = w_q
            nc.tensor.matmul_mx(
                out=acc,
                lhsT=codes[:, g * N : (g + 1) * N].bitcast(FP8X4),
                lhsT_scale=scales[:, g * N : (g + 1) * N],
                rhs=x_codes[g][:, lo:hi].bitcast(FP8X4),
                rhs_scale=x_planes[4 * g : P, lo:hi],
                start=(g == 0),
                stop=(g == PASSES - 1),
            )

        ys = {lo: ps.tile([P, hi - lo], F32, name="ys%d" % lo) for half in YS_PIECES for lo, hi in half}
        nc.vector.tensor_copy(x_codes[0][:], word_tables[0][:].bitcast(U32).indirect(offsets[:]))
        nc.vector.tensor_copy(x_planes[:], scale_table[:].indirect(offsets[:]))
        buys_sb = sb.tile([P, S], F32, name="buys_sb", tag="slot_table0", align_bytes=64)
        nc.sync.dma_start(buys_sb[:], buys)
        for half in YS_PIECES:
            for lo, hi in half:
                product_pass(ys[lo][:], w3_q, 0, lo, hi)

        spent = sb.tile([P, S], F32, name="spent")
        nc.scalar.activation(spent[:], logv_sb[:], ACT.Exp, scale=0.5)

        x_codes.append(sb.tile([P, S], U32, name="x_codes1", tag="slot_c", align_bytes=64))
        exp_ys = sb.tile([P, S], F32, name="exp_ys")
        for h in range(2):
            lo, hi = h * HALF, (h + 1) * HALF
            nc.vector.tensor_copy(
                x_codes[1][:, lo:hi],
                word_tables[1][:].bitcast(U32).indirect(offsets[:, lo // 16 : hi // 16]),
            )
            for lo, hi in YS_PIECES[h]:
                product_pass(ys[lo][:], w3_q, 1, lo, hi)
                nc.scalar.activation(exp_ys[:, lo:hi], ys[lo][:], ACT.Exp)

        softplus = logv_sb
        nc.scalar.activation(softplus[:], exp_ys[:], ACT.Ln, bias=1.0)

        ym = ps.tile([P, S], F32, name="ym")
        w2_q = quantise_weight(w2_raw, "w2", "slot_table1", nc.vector.tensor_copy)
        for g in range(PASSES):
            product_pass(ym[:], w2_q, g, 0, S)
        yp = ps.tile([P, S], F32, name="yp")
        w1_q = quantise_weight(w1_raw, "w1", "slot_table1", nc.vector.tensor_copy)
        for g in range(PASSES):
            product_pass(yp[:], w1_q, g, 0, S)

        quad = sb.tile([P, S], F32, name="quad", tag="slot_table1", align_bytes=64)
        expo = sb.tile([P, S], F32, name="expo")
        halves = [slice(h * HALF, (h + 1) * HALF) for h in range(2)]
        for c in halves:
            nc.vector.scalar_tensor_tensor(quad[:, c], softplus[:, c], LIN, softplus[:, c], ALU.add, ALU.mult)
        for c in halves:
            nc.vector.scalar_tensor_tensor(expo[:, c], ym[:, c], 0.5 / SQ, quad[:, c], ALU.mult, ALU.add)

        seen = sb.tile([P, S], F32, name="seen", tag="slot_table1", align_bytes=64)
        nc.vector.tensor_tensor(seen[:], spent[:], buys_sb[:], ALU.mult)

        gate = sb.tile([P, S], F32, name="gate")
        value = sb.tile([P, S], F32, name="value")
        gated = sb.tile([P, S], F32, name="gated")
        result = sb.tile([P, S], F32, name="result")
        for lo, hi in TAIL:
            c = slice(lo, hi)
            nc.scalar.activation(gate[:, c], yp[:, c], ACT.Tanh, scale=0.5)
            nc.scalar.activation(value[:, c], expo[:, c], ACT.Exp, scale=SQ)
            nc.vector.scalar_tensor_tensor(gated[:, c], gate[:, c], 1.0, value[:, c], ALU.add, ALU.mult)
            nc.vector.scalar_tensor_tensor(result[:, c], gated[:, c], OUT_SCALE, seen[:, c], ALU.mult, ALU.subtract)
            nc.sync.dma_start(out[:, c], result[:, c])
